import numpy as np
import ml_dtypes


def mxq(x, axis, fmt="e4m3"):
    dtype, down = {"e4m3": (ml_dtypes.float8_e4m3fn, 7), "e5m2": (ml_dtypes.float8_e5m2, 14)}[fmt]
    v = np.moveaxis(np.asarray(x, np.float32).astype(ml_dtypes.bfloat16).astype(np.float64), axis, -1)
    blocks = v.reshape(v.shape[:-1] + (-1, 32))
    amax = np.abs(blocks).max(-1, keepdims=True)
    byte = np.maximum(np.where(amax > 0, np.frexp(amax)[1] - 1 + 127, 0) - down, 1)
    scale = np.exp2(byte - 127.0)
    codes = (blocks / scale).astype(np.float32).astype(dtype).astype(np.float64)
    return np.moveaxis((codes * scale).reshape(v.shape), -1, axis)


WIDE = False


def mx_kscale(k):
    if not WIDE:
        return np.ones(k)
    levels = np.array([10, -10, 5, -5, 0])
    if k % 512:
        return np.exp2(np.random.permutation(np.resize(levels, k // 32))).repeat(32)
    a = np.empty((k // 512, 16))
    for p in range(k // 512):
        a[p, :8] = np.random.permutation(np.resize(levels, 8))
        for g in range(8):
            far = levels[np.abs(levels - a[p, g]) >= 10]
            a[p, g + 8] = far[np.random.randint(len(far))]
    return np.exp2(a.ravel()).repeat(32)


def f64(x):
    return np.asarray(x).astype(np.float64)


def striped(idx):
    return np.tile(idx.reshape(-1, 16).T, (8, 1)).astype(np.uint16)


def unstriped(offs):
    return offs[:16].T.reshape(-1).astype(np.int64)


def striped8(idx):
    return np.concatenate([x.reshape(-1, 16).T for x in idx]).astype(np.uint16)


def runs(offs, k):
    lists = np.stack([offs[16 * r : 16 * r + 16].T.reshape(-1) for r in range(8)]).astype(np.int64)
    return lists[np.arange(k) % 512 // 64]


def pack_weight(w):
    k, n = w.shape
    w = f64(np.asarray(w, np.float32).astype(ml_dtypes.bfloat16)).reshape(k // 32, 32, n)
    amax = np.abs(w).max(1)
    byte = np.clip(np.where(amax > 0, np.frexp(amax)[1] - 1 + 127 - 7, 1), 1, 254)
    scaled = (w * np.exp2(127.0 - byte)[:, None, :]).reshape(k, n).astype(np.float32)
    words = np.ascontiguousarray(scaled.reshape(k // 512, 128, 4, n).transpose(0, 1, 3, 2)).astype(ml_dtypes.float8_e4m3fn).view(np.uint8)
    return words, np.ascontiguousarray(byte.astype(np.uint8).reshape(k // 512, 16, n))


def unpack_weight(words, scales):
    g, p, n, _ = words.shape
    vals = np.ascontiguousarray(words).view(ml_dtypes.float8_e4m3fn).astype(np.float64) * np.repeat(np.exp2(scales.astype(np.float64) - 127.0), 8, axis=1)[..., None]
    return vals.transpose(0, 1, 3, 2).reshape(g * 512, n)


def sigmoid(v):
    return 1.0 / (1.0 + np.exp(-np.maximum(v, -700.0)))


K, T, S, N, H, W, U = 512, 2048, 256, 512, 512, 1024, 1024


def setup_inputs():
    n = np.random.standard_normal
    s = mx_kscale(K)[:, None]
    u = mx_kscale(H)
    packed_xT = pack_weight(n((K, T)) * s)
    return {
        "x_words": packed_xT[0],
        "x_scales": packed_xT[1],
        "w1": (n((K, H)) / np.sqrt(K) / s).astype(np.float32),
        "gn": (np.random.uniform(0.5, 1.5, (H, 1)) * u[:, None]).astype(np.float32),
        "w2": (n((H, N)) / np.sqrt(H) / u[:, None]).astype(np.float32),
        "mem": n((N, U)).astype(np.float32),
        "sl": np.random.uniform(1.0, 2.0, (N, 1)).astype(np.float32),
        "th": (0.5 * n((N, 1))).astype(np.float32),
        "offs": striped8(np.random.randint(0, T, (8, S))),
        "n1": striped(np.random.randint(0, S, W)),
        "n2": striped(np.random.permutation(U)[:S]),
        "n3": striped(np.random.permutation(S)),
    }


def reference(x_words, x_scales, w1, gn, w2, mem, sl, th, offs, n1, n2, n3):
    old = f64(mem)[:, unstriped(n2)]
    xq = unpack_weight(x_words, x_scales)[np.arange(K)[:, None], runs(offs, K)]
    y = mxq(f64(w1), 0, "e4m3").T @ xq
    mb = y[:, unstriped(n1)]
    ms = mb.reshape(H, S, 4).sum(axis=2)
    z = f64(gn) * (y * sigmoid(ms))
    h = mxq(f64(w2), 0, "e4m3").T @ mxq(z, 0, "e4m3")
    sg = sigmoid(f64(sl) * (h[:, unstriped(n3)] - f64(th)))
    nw = old + sg * (h - old)
    out = f64(mem).copy()
    out[:, unstriped(n2)] = nw
    return out

@@ -1,0 +1,285 @@
+from contextlib import ExitStack
+
+import concourse.mybir as mybir
+
+K, T, S, N, H, W, U = 512, 2048, 256, 512, 512, 1024, 1024
+FLOPS = 2 * K * H * S + 2 * H * N * S
+
+F32 = mybir.dt.float32
+BF16 = mybir.dt.bfloat16
+I32 = mybir.dt.int32
+U32 = mybir.dt.uint32
+U16 = mybir.dt.uint16
+U8 = mybir.dt.uint8
+FP8X4 = mybir.dt.float8_e4m3fn_x4
+ADD = mybir.AluOpType.add
+SUB = mybir.AluOpType.subtract
+MULT = mybir.AluOpType.mult
+COPY = mybir.ActivationFunctionType.Copy
+SIGMOID = mybir.ActivationFunctionType.Sigmoid
+
+P = 128
+PACK = 4
+MEMBERS = 4
+HALF = S // 2
+HALF_ENTRIES = HALF * MEMBERS
+LIST_ROWS = 16
+Y_WINDOW = HALF_ENTRIES + LIST_ROWS
+H_WINDOW = 2 * S
+VECTOR_GATHER_TILE = 1
+VECTOR_SCATTER_TILES = (0, 3)
+
+
+def tile_picked_hashgsumgepg_none_p_kernel(
+    tc, x_words, x_scales, w1, gn, w2, mem, sl, th, offs, n1, n2, n3, out
+):
+    nc = tc.nc
+    with ExitStack() as ctx:
+        keep = ctx.enter_context(tc.tile_pool(name="keep", bufs=1))
+        shared = ctx.enter_context(tc.tile_pool(name="shared", bufs=1))
+        reused = ctx.enter_context(tc.tile_pool(name="reused", bufs=1))
+        psum = ctx.enter_context(tc.psum_pool(name="psum", bufs=1))
+
+        offs_t = keep.tile([P, S // LIST_ROWS], U16, name="offs_t")
+        n1_t = keep.tile([P, W // LIST_ROWS], U16, name="n1_t")
+        n2_t = keep.tile([P, S // LIST_ROWS], U16, name="n2_t")
+        n3_t = keep.tile([P, S // LIST_ROWS], U16, name="n3_t")
+
+        w1_raw = shared.tile([P, PACK, H], F32, name="w1_raw", offset=0, align_bytes=64)
+        x_window = shared.tile([P, T], U32, name="x_window", offset=8192, align_bytes=64)
+        scale_window = shared.tile([P, T], U8, name="scale_window", offset=16384, align_bytes=64)
+        picked_scales = shared.tile([P, S], U8, name="picked_scales", offset=20480, align_bytes=64)
+
+        nc.vector.memset(scale_window[:].bitcast(I32), 0)
+        nc.sync.dma_start(offs_t[:], offs)
+        for e in range(2):
+            nc.scalar.dma_start(scale_window[e:P:LIST_ROWS, :].bitcast(I32), x_scales[0, e:16:2, :].bitcast(I32))
+        nc.sync.dma_start(w1_raw[:], w1.rearrange("(p j) c -> p j c", j=PACK))
+        nc.sync.dma_start(x_window[:].bitcast(I32), x_words[0].rearrange("p n t -> p (n t)").bitcast(I32))
+        nc.sync.dma_start(n1_t[:], n1)
+        nc.sync.dma_start(n2_t[:], n2)
+        nc.sync.dma_start(n3_t[:], n3)
+
+        gn_t = keep.tile([P, PACK], F32, name="gn_t")
+        sl_t = keep.tile([P, PACK], F32, name="sl_t")
+        th_t = keep.tile([P, PACK], F32, name="th_t")
+        nc.gpsimd.dma_start(gn_t[:], gn.rearrange("(p t) o -> p (t o)", t=PACK))
+        with nc.allow_non_contiguous_dma(reason="one value a row of h"):
+            nc.gpsimd.dma_start(sl_t[:], sl.rearrange("(m p) o -> p (m o)", p=P))
+            nc.gpsimd.dma_start(th_t[:], th.rearrange("(m p) o -> p (m o)", p=P))
+
+        y = [keep.tile([P, Y_WINDOW], F32, name="y%d" % t) for t in range(PACK)]
+        h = [keep.tile([P, H_WINDOW], F32, name="h%d" % m) for m in range(PACK)]
+
+        nc.vector.tensor_copy(picked_scales[:], scale_window[:].indirect(offs_t[:]))
+        x_plane = keep.tile([P, S], U8, name="x_plane", align_bytes=64)
+        nc.vector.tensor_copy(x_plane[:].bitcast(I32), picked_scales[:].bitcast(I32))
+        for e in range(2):
+            nc.scalar.dma_start(x_plane[2 + e : P : 32, :].bitcast(I32), picked_scales[16 + e : P : 32, :].bitcast(I32))
+
+        for t in range(PACK):
+            nc.gpsimd.memset(y[t][:, S:], 0.0)
+        for m in range(PACK):
+            nc.gpsimd.memset(h[m][:, S:], 0.0)
+
+        w1_grouped = shared.tile([P, PACK * H], BF16, name="w1_grouped", offset=16384, align_bytes=64)
+        nc.vector.tensor_copy(
+            w1_grouped[:].rearrange("p (t m j) -> p m j t", t=PACK, j=PACK),
+            w1_raw[:].rearrange("p j (m t) -> p m j t", t=PACK),
+        )
+        w1_codes = keep.tile([P, H], U32, name="w1_codes", align_bytes=64)
+        w1_plane = keep.tile([P, H], U8, name="w1_plane", align_bytes=64)
+        nc.vector.quantize_mx(out=w1_codes[:].bitcast(FP8X4), scales=w1_plane[:], in_=w1_grouped[:])
+
+        x_codes = keep.tile([P, S], U32, name="x_codes", align_bytes=64)
+        nc.vector.tensor_copy(x_codes[:], x_window[:].indirect(offs_t[:]))
+
+        w2_raw = shared.tile([P, PACK, N], F32, name="w2_raw", offset=0, align_bytes=64)
+        nc.sync.dma_start(w2_raw[:], w2.rearrange("(p j) c -> p j c", j=PACK))
+        page_offsets = (16384, 20480, 8192, 12288)
+        page = [
+            shared.tile([P, U], F32, name="page%d" % m, offset=page_offsets[m], align_bytes=64) for m in range(PACK)
+        ]
+        for m in range(PACK):
+            nc.sync.dma_start(page[m][:], mem[m * P : (m + 1) * P, :])
+
+        for t in range(PACK):
+            cols = slice(t * P, (t + 1) * P)
+            y_bank = psum.tile([P, S], F32, name="y_bank%d" % t)
+            nc.tensor.matmul_mx(
+                out=y_bank[:],
+                lhsT=w1_codes[:, cols].bitcast(FP8X4),
+                lhsT_scale=w1_plane[:, cols],
+                rhs=x_codes[:].bitcast(FP8X4),
+                rhs_scale=x_plane[:],
+                start=True,
+                stop=True,
+            )
+            if t == 0:
+                nc.scalar.copy(y[t][:, :S], y_bank[:])
+            else:
+                nc.vector.tensor_copy(y[t][:, :S], y_bank[:])
+
+        w2_grouped = keep.tile([P, N, PACK], BF16, name="w2_grouped", align_bytes=64)
+        nc.gpsimd.tensor_scalar(w2_grouped[:], w2_raw[:].rearrange("p j c -> p c j"), 1.0, 0.0, MULT, ADD)
+        w2_plane = keep.tile([P, N], U8, name="w2_plane", align_bytes=64)
+
+        members = {}
+        member_offsets = {(0, 3): 0, (1, 2): 2048}
+
+        def gather_members(half, t):
+            list_cols = HALF_ENTRIES // LIST_ROWS
+            if (half, t) in member_offsets:
+                members[half, t] = reused.tile(
+                    [P, HALF_ENTRIES], F32, name="members%d_%d" % (half, t), offset=member_offsets[half, t], align_bytes=64
+                )
+            else:
+                members[half, t] = keep.tile([P, HALF_ENTRIES], F32, name="members%d_%d" % (half, t))
+            looked_up = y[t][:].indirect(n1_t[:, half * list_cols : (half + 1) * list_cols])
+            if t == VECTOR_GATHER_TILE:
+                nc.vector.tensor_copy(members[half, t][:], looked_up)
+            else:
+                nc.scalar.activation(members[half, t][:], looked_up, COPY)
+
+        z_codes = keep.tile([P, S], U32, name="z_codes", align_bytes=64)
+        z_plane = keep.tile([P, S], U8, name="z_plane", align_bytes=64)
+        h_banks = [psum.tile([P, S], F32, name="h_bank%d" % m) for m in range(PACK)]
+
+        pairs = {}
+        sig = {}
+        ms = [reused.tile([P, PACK, HALF], F32, name="ms%d" % half, offset=2048 * (half + 1), align_bytes=64) for half in range(2)]
+        z_rows = [keep.tile([P, PACK, HALF], BF16, name="z_rows%d" % half) for half in range(2)]
+        z_grouped = [keep.tile([P, HALF, PACK], BF16, name="z_grouped%d" % half, align_bytes=64) for half in range(2)]
+
+        def add_pairs(half, t):
+            pairs[half, t] = keep.tile([P, HALF, 2], F32, name="pairs%d_%d" % (half, t))
+            grouped = members[half, t][:].rearrange("p (j a b) -> p j a b", a=2, b=2)
+            nc.vector.tensor_tensor(pairs[half, t][:], grouped[:, :, 0, :], grouped[:, :, 1, :], ADD)
+
+        def sum_and_sigmoid(half, t):
+            nc.vector.tensor_tensor(ms[half][:, t, :], pairs[half, t][:, :, 0], pairs[half, t][:, :, 1], ADD)
+            sig[half, t] = keep.tile([P, HALF], F32, name="sig%d_%d" % (half, t))
+            nc.scalar.activation(sig[half, t][:], ms[half][:, t, :], SIGMOID)
+
+        def gate(half, t):
+            cols = slice(half * HALF, (half + 1) * HALF)
+            nc.vector.scalar_tensor_tensor(
+                z_rows[half][:, t, :], y[t][:, cols], gn_t[:, t : t + 1], sig[half, t][:], MULT, MULT
+            )
+
+        def interleave(half):
+            nc.vector.tensor_copy(z_grouped[half][:], z_rows[half][:].rearrange("p t j -> p j t"))
+
+        def quantize_z(half):
+            cols = slice(half * HALF, (half + 1) * HALF)
+            nc.vector.quantize_mx(
+                out=z_codes[:, cols].bitcast(FP8X4),
+                scales=z_plane[:, cols],
+                in_=z_grouped[half][:].rearrange("p j t -> p (j t)"),
+            )
+
+        def second_product(half):
+            cols = slice(half * HALF, (half + 1) * HALF)
+            for m in range(PACK):
+                rows = slice(m * P, (m + 1) * P)
+                nc.tensor.matmul_mx(
+                    out=h_banks[m][:, cols],
+                    lhsT=w2_codes[:, rows].bitcast(FP8X4),
+                    lhsT_scale=w2_plane[:, rows],
+                    rhs=z_codes[:, cols].bitcast(FP8X4),
+                    rhs_scale=z_plane[:, cols],
+                    start=True,
+                    stop=True,
+                )
+
+        for t in range(PACK):
+            gather_members(0, t)
+        gather_members(1, 1)
+        gather_members(1, 0)
+        add_pairs(0, 0)
+        add_pairs(0, 1)
+        sum_and_sigmoid(0, 0)
+        add_pairs(0, 2)
+        sum_and_sigmoid(0, 1)
+        add_pairs(0, 3)
+        sum_and_sigmoid(0, 2)
+        add_pairs(1, 1)
+        sum_and_sigmoid(0, 3)
+        add_pairs(1, 0)
+        sum_and_sigmoid(1, 1)
+        gate(0, 0)
+        sum_and_sigmoid(1, 0)
+        gather_members(1, 2)
+        gather_members(1, 3)
+        gate(0, 1)
+        gate(0, 2)
+        gate(0, 3)
+        w2_codes = reused.tile([P, N], U32, name="w2_codes", offset=0, align_bytes=64)
+        nc.vector.quantize_mx(
+            out=w2_codes[:].bitcast(FP8X4), scales=w2_plane[:], in_=w2_grouped[:].rearrange("p c j -> p (c j)")
+        )
+        interleave(0)
+        gate(1, 1)
+        quantize_z(0)
+        second_product(0)
+        add_pairs(1, 2)
+        gate(1, 0)
+        sum_and_sigmoid(1, 2)
+        add_pairs(1, 3)
+        gate(1, 2)
+        sum_and_sigmoid(1, 3)
+        gate(1, 3)
+        interleave(1)
+        quantize_z(1)
+        second_product(1)
+
+        bias = keep.tile([P, PACK], F32, name="bias")
+        nc.vector.scalar_tensor_tensor(bias[:], sl_t[:], -1.0, th_t[:], MULT, MULT)
+
+        old = reused.tile([P, PACK, S], F32, name="old", offset=4096, align_bytes=64)
+        for m in range(PACK):
+            nc.scalar.activation(old[:, m, :], page[m][:].indirect(n2_t[:]), COPY)
+
+        sg = [keep.tile([P, S], F32, name="sg%d" % m) for m in range(PACK)]
+        change = [keep.tile([P, S], F32, name="change%d" % m) for m in range(PACK)]
+        gated = [keep.tile([P, S], F32, name="gated%d" % m) for m in range(PACK)]
+        nw = {m: keep.tile([P, S], F32, name="nw%d" % m) for m in (1, 2)}
+        for m in range(PACK):
+            if m == 1:
+                nc.vector.tensor_copy(h[m][:, :S], h_banks[m][:])
+            else:
+                nc.scalar.copy(h[m][:, :S], h_banks[m][:])
+            nc.scalar.activation(
+                sg[m][:], h[m][:].indirect(n3_t[:]), SIGMOID, bias=bias[:, m : m + 1], scale=sl_t[:, m : m + 1]
+            )
+
+        def subtract_old(m):
+            nc.vector.tensor_tensor(change[m][:], h[m][:, :S], old[:, m, :], SUB)
+
+        def apply_gate(m):
+            nc.vector.tensor_tensor(gated[m][:], sg[m][:], change[m][:], MULT)
+
+        def add_old(m):
+            nc.vector.tensor_tensor(nw[m][:], gated[m][:], old[:, m, :], ADD)
+
+        def scatter_and_store(m):
+            if m in VECTOR_SCATTER_TILES:
+                nc.vector.tensor_tensor(page[m][:].indirect(n2_t[:]), gated[m][:], old[:, m, :], ADD)
+            else:
+                nc.scalar.activation(page[m][:].indirect(n2_t[:]), nw[m][:], COPY)
+            nc.sync.dma_start(out[m * P : (m + 1) * P, :], page[m][:])
+
+        subtract_old(0)
+        subtract_old(1)
+        apply_gate(0)
+        apply_gate(1)
+        subtract_old(2)
+        add_old(1)
+        scatter_and_store(0)
+        scatter_and_store(1)
+        apply_gate(2)
+        subtract_old(3)
+        add_old(2)
+        apply_gate(3)
+        scatter_and_store(2)
+        scatter_and_store(3)

@@ -1,6 +1,7 @@
 from contextlib import ExitStack
 
 import concourse.mybir as mybir
+from concourse.masks import make_identity
 
 K, T, S, N, H, W, U = 512, 2048, 256, 512, 512, 1024, 1024
 FLOPS = 2 * K * H * S + 2 * H * N * S
@@ -15,6 +16,7 @@ FP8X4 = mybir.dt.float8_e4m3fn_x4
 ADD = mybir.AluOpType.add
 SUB = mybir.AluOpType.subtract
 MULT = mybir.AluOpType.mult
+AXIS_X = mybir.AxisListType.X
 COPY = mybir.ActivationFunctionType.Copy
 SIGMOID = mybir.ActivationFunctionType.Sigmoid
 
@@ -26,8 +28,10 @@ HALF_ENTRIES = HALF * MEMBERS
 LIST_ROWS = 16
 Y_WINDOW = HALF_ENTRIES + LIST_ROWS
 H_WINDOW = 2 * S
-VECTOR_GATHER_TILE = 1
-VECTOR_SCATTER_TILES = (0, 3)
+VECTOR_GATHERS = ((0, 1), (1, 1), (1, 2))
+W1_VECTOR_SHARE = 88
+X_CODES_AT = 16384 + 64 + 4096 + 4096 - 256
+VECTOR_SCATTER_TILES = (2, 3)
 
 
 def tile_picked_hashgsumgepg_none_p_kernel(
@@ -47,65 +51,72 @@ def tile_picked_hashgsumgepg_none_p_kernel(
 
         w1_raw = shared.tile([P, PACK, H], F32, name="w1_raw", offset=0, align_bytes=64)
         x_window = shared.tile([P, T], U32, name="x_window", offset=8192, align_bytes=64)
-        scale_window = shared.tile([P, T], U8, name="scale_window", offset=16384, align_bytes=64)
-        picked_scales = shared.tile([P, S], U8, name="picked_scales", offset=20480, align_bytes=64)
+        scale_window = keep.tile([P, T], U8, name="scale_window", align_bytes=64)
+        picked_scales = shared.tile([P, S], U8, name="picked_scales", offset=16384, align_bytes=64)
 
-        nc.vector.memset(scale_window[:].bitcast(I32), 0)
+        warm_in = keep.tile([P, 1], F32, name="warm_in")
+        warm_out = keep.tile([P, 1], F32, name="warm_out")
+        nc.gpsimd.memset(warm_in[:], 0.0)
+        nc.scalar.activation(warm_out[:], warm_in[:], SIGMOID)
+
         nc.sync.dma_start(offs_t[:], offs)
-        for e in range(2):
-            nc.scalar.dma_start(scale_window[e:P:LIST_ROWS, :].bitcast(I32), x_scales[0, e:16:2, :].bitcast(I32))
+        nc.sync.dma_start(
+            scale_window[:].bitcast(I32), x_scales[0].bitcast(I32).unsqueeze(1).to_broadcast([16, 8, T // 4])
+        )
         nc.sync.dma_start(w1_raw[:], w1.rearrange("(p j) c -> p j c", j=PACK))
         nc.sync.dma_start(x_window[:].bitcast(I32), x_words[0].rearrange("p n t -> p (n t)").bitcast(I32))
         nc.sync.dma_start(n1_t[:], n1)
         nc.sync.dma_start(n2_t[:], n2)
         nc.sync.dma_start(n3_t[:], n3)
 
-        gn_t = keep.tile([P, PACK], F32, name="gn_t")
-        sl_t = keep.tile([P, PACK], F32, name="sl_t")
-        th_t = keep.tile([P, PACK], F32, name="th_t")
-        nc.gpsimd.dma_start(gn_t[:], gn.rearrange("(p t) o -> p (t o)", t=PACK))
-        with nc.allow_non_contiguous_dma(reason="one value a row of h"):
-            nc.gpsimd.dma_start(sl_t[:], sl.rearrange("(m p) o -> p (m o)", p=P))
-            nc.gpsimd.dma_start(th_t[:], th.rearrange("(m p) o -> p (m o)", p=P))
+        identity = keep.tile([P, P], F32, name="identity")
+        make_identity(nc, identity[:])
 
         y = [keep.tile([P, Y_WINDOW], F32, name="y%d" % t) for t in range(PACK)]
         h = [keep.tile([P, H_WINDOW], F32, name="h%d" % m) for m in range(PACK)]
 
+        for t in range(PACK):
+            nc.vector.memset(y[t][:, S:], 0.0)
+        for m in range(PACK):
+            nc.vector.memset(h[m][:, S:], 0.0)
+
         nc.vector.tensor_copy(picked_scales[:], scale_window[:].indirect(offs_t[:]))
         x_plane = keep.tile([P, S], U8, name="x_plane", align_bytes=64)
         nc.vector.tensor_copy(x_plane[:].bitcast(I32), picked_scales[:].bitcast(I32))
-        for e in range(2):
-            nc.scalar.dma_start(x_plane[2 + e : P : 32, :].bitcast(I32), picked_scales[16 + e : P : 32, :].bitcast(I32))
+        for c in range(1, 4):
+            nc.scalar.dma_start(x_plane[c:P:32, :].bitcast(I32), picked_scales[8 * c : P : 32, :].bitcast(I32))
 
-        for t in range(PACK):
-            nc.gpsimd.memset(y[t][:, S:], 0.0)
-        for m in range(PACK):
-            nc.gpsimd.memset(h[m][:, S:], 0.0)
-
-        w1_grouped = shared.tile([P, PACK * H], BF16, name="w1_grouped", offset=16384, align_bytes=64)
-        nc.vector.tensor_copy(
-            w1_grouped[:].rearrange("p (t m j) -> p m j t", t=PACK, j=PACK),
-            w1_raw[:].rearrange("p j (m t) -> p m j t", t=PACK),
-        )
+        w1_grouped = keep.tile([P, PACK * H], BF16, name="w1_grouped", align_bytes=64)
+        dealt = w1_grouped[:].rearrange("p (t m j) -> p m t j", t=PACK, j=PACK)
+        source = w1_raw[:].rearrange("p j (m t) -> p m t j", t=PACK)
+        nc.vector.tensor_copy(dealt[:, :W1_VECTOR_SHARE], source[:, :W1_VECTOR_SHARE])
+        nc.scalar.copy(dealt[:, W1_VECTOR_SHARE:], source[:, W1_VECTOR_SHARE:])
         w1_codes = keep.tile([P, H], U32, name="w1_codes", align_bytes=64)
         w1_plane = keep.tile([P, H], U8, name="w1_plane", align_bytes=64)
         nc.vector.quantize_mx(out=w1_codes[:].bitcast(FP8X4), scales=w1_plane[:], in_=w1_grouped[:])
 
-        x_codes = keep.tile([P, S], U32, name="x_codes", align_bytes=64)
+        x_codes = shared.tile([P, S], U32, name="x_codes", offset=X_CODES_AT, align_bytes=64)
         nc.vector.tensor_copy(x_codes[:], x_window[:].indirect(offs_t[:]))
 
+        gn_t = shared.tile([P, PACK], F32, name="gn_t", offset=16384, align_bytes=64)
+        sl_t = shared.tile([P, PACK], F32, name="sl_t", offset=X_CODES_AT + 256, align_bytes=64)
+        th_t = shared.tile([P, PACK], F32, name="th_t", offset=X_CODES_AT + 320, align_bytes=64)
         w2_raw = shared.tile([P, PACK, N], F32, name="w2_raw", offset=0, align_bytes=64)
-        nc.sync.dma_start(w2_raw[:], w2.rearrange("(p j) c -> p j c", j=PACK))
-        page_offsets = (16384, 20480, 8192, 12288)
+        page_offsets = (16384 + 64, 8192, 12288, X_CODES_AT + 256 - 4096)
         page = [
             shared.tile([P, U], F32, name="page%d" % m, offset=page_offsets[m], align_bytes=64) for m in range(PACK)
         ]
+        nc.sync.dma_start(w2_raw[:], w2.rearrange("(p j) c -> p j c", j=PACK))
+        nc.sync.dma_start(gn_t[:], gn.rearrange("(p t) o -> p (t o)", t=PACK))
         for m in range(PACK):
             nc.sync.dma_start(page[m][:], mem[m * P : (m + 1) * P, :])
+        with nc.allow_non_contiguous_dma(reason="one value a row of h"):
+            nc.sync.dma_start(sl_t[:], sl.rearrange("(m p) o -> p (m o)", p=P))
+            nc.sync.dma_start(th_t[:], th.rearrange("(m p) o -> p (m o)", p=P))
 
         for t in range(PACK):
             cols = slice(t * P, (t + 1) * P)
-            y_bank = psum.tile([P, S], F32, name="y_bank%d" % t)
+            y_bank = psum.tile([P, S], F32, name="y_bank%d" % t, tag="bank%d" % t)
             nc.tensor.matmul_mx(
                 out=y_bank[:],
                 lhsT=w1_codes[:, cols].bitcast(FP8X4),
@@ -115,51 +126,57 @@ def tile_picked_hashgsumgepg_none_p_kernel(
                 start=True,
                 stop=True,
             )
-            if t == 0:
+            if t % 2 == 0:
                 nc.scalar.copy(y[t][:, :S], y_bank[:])
             else:
                 nc.vector.tensor_copy(y[t][:, :S], y_bank[:])
 
-        w2_grouped = keep.tile([P, N, PACK], BF16, name="w2_grouped", align_bytes=64)
-        nc.gpsimd.tensor_scalar(w2_grouped[:], w2_raw[:].rearrange("p j c -> p c j"), 1.0, 0.0, MULT, ADD)
+        w2_codes = keep.tile([P, N], U32, name="w2_codes", align_bytes=64)
         w2_plane = keep.tile([P, N], U8, name="w2_plane", align_bytes=64)
 
         members = {}
-        member_offsets = {(0, 3): 0, (1, 2): 2048}
 
         def gather_members(half, t):
             list_cols = HALF_ENTRIES // LIST_ROWS
-            if (half, t) in member_offsets:
-                members[half, t] = reused.tile(
-                    [P, HALF_ENTRIES], F32, name="members%d_%d" % (half, t), offset=member_offsets[half, t], align_bytes=64
-                )
-            else:
-                members[half, t] = keep.tile([P, HALF_ENTRIES], F32, name="members%d_%d" % (half, t))
+            members[half, t] = keep.tile([P, HALF_ENTRIES], F32, name="members%d_%d" % (half, t))
             looked_up = y[t][:].indirect(n1_t[:, half * list_cols : (half + 1) * list_cols])
-            if t == VECTOR_GATHER_TILE:
+            if (half, t) in VECTOR_GATHERS:
                 nc.vector.tensor_copy(members[half, t][:], looked_up)
             else:
                 nc.scalar.activation(members[half, t][:], looked_up, COPY)
 
         z_codes = keep.tile([P, S], U32, name="z_codes", align_bytes=64)
         z_plane = keep.tile([P, S], U8, name="z_plane", align_bytes=64)
-        h_banks = [psum.tile([P, S], F32, name="h_bank%d" % m) for m in range(PACK)]
+        h_banks = {}
 
-        pairs = {}
         sig = {}
-        ms = [reused.tile([P, PACK, HALF], F32, name="ms%d" % half, offset=2048 * (half + 1), align_bytes=64) for half in range(2)]
-        z_rows = [keep.tile([P, PACK, HALF], BF16, name="z_rows%d" % half) for half in range(2)]
+        sums = {}
+        z_rows = [
+            shared.tile([P, PACK, HALF], BF16, name="z_rows%d" % half, offset=4096 + 1024 * half, align_bytes=64)
+            for half in range(2)
+        ]
         z_grouped = [keep.tile([P, HALF, PACK], BF16, name="z_grouped%d" % half, align_bytes=64) for half in range(2)]
 
-        def add_pairs(half, t):
-            pairs[half, t] = keep.tile([P, HALF, 2], F32, name="pairs%d_%d" % (half, t))
-            grouped = members[half, t][:].rearrange("p (j a b) -> p j a b", a=2, b=2)
-            nc.vector.tensor_tensor(pairs[half, t][:], grouped[:, :, 0, :], grouped[:, :, 1, :], ADD)
+        def sum_on_vector(half, t, ms):
+            nc.vector.tensor_reduce(ms, members[half, t][:].rearrange("p (j a) -> p j a", a=MEMBERS), AXIS_X, ADD)
 
-        def sum_and_sigmoid(half, t):
-            nc.vector.tensor_tensor(ms[half][:, t, :], pairs[half, t][:, :, 0], pairs[half, t][:, :, 1], ADD)
+        def sigmoid_in_place(half, t, ms):
             sig[half, t] = keep.tile([P, HALF], F32, name="sig%d_%d" % (half, t))
-            nc.scalar.activation(sig[half, t][:], ms[half][:, t, :], SIGMOID)
+            nc.scalar.activation(sig[half, t][:], ms, SIGMOID)
+
+        def sum_on_tensor(half, t, bank):
+            sums[half, t] = psum.tile([P, P], F32, name="sum%d_%d" % (half, t), tag="bank%d" % bank)
+            by_member = members[half, t][:].rearrange("p (j a) -> p a j", a=MEMBERS)
+            for a in range(MEMBERS):
+                nc.tensor.matmul(
+                    sums[half, t][:], by_member[:, a, :], identity[:], start=a == 0, stop=a == MEMBERS - 1, is_transpose=True
+                )
+
+        def sigmoid_and_back(half, t, bank):
+            turned = keep.tile([P, P], F32, name="turned%d_%d" % (half, t))
+            nc.scalar.activation(turned[:], sums[half, t][:], SIGMOID)
+            sig[half, t] = psum.tile([P, HALF], F32, name="sig%d_%d" % (half, t), tag="bank%d" % bank)
+            nc.tensor.transpose(sig[half, t][:], turned[:], identity[:])
 
         def gate(half, t):
             cols = slice(half * HALF, (half + 1) * HALF)
@@ -178,77 +195,77 @@ def tile_picked_hashgsumgepg_none_p_kernel(
                 in_=z_grouped[half][:].rearrange("p j t -> p (j t)"),
             )
 
-        def second_product(half):
-            cols = slice(half * HALF, (half + 1) * HALF)
-            for m in range(PACK):
-                rows = slice(m * P, (m + 1) * P)
-                nc.tensor.matmul_mx(
-                    out=h_banks[m][:, cols],
-                    lhsT=w2_codes[:, rows].bitcast(FP8X4),
-                    lhsT_scale=w2_plane[:, rows],
-                    rhs=z_codes[:, cols].bitcast(FP8X4),
-                    rhs_scale=z_plane[:, cols],
-                    start=True,
-                    stop=True,
-                )
-
+        ms_early = keep.tile([P, HALF], F32, name="ms_early")
+        ms_late = shared.tile([P, 2, HALF], F32, name="ms_late", offset=0, align_bytes=64)
         for t in range(PACK):
             gather_members(0, t)
         gather_members(1, 1)
-        gather_members(1, 0)
-        add_pairs(0, 0)
-        add_pairs(0, 1)
-        sum_and_sigmoid(0, 0)
-        add_pairs(0, 2)
-        sum_and_sigmoid(0, 1)
-        add_pairs(0, 3)
-        sum_and_sigmoid(0, 2)
-        add_pairs(1, 1)
-        sum_and_sigmoid(0, 3)
-        add_pairs(1, 0)
-        sum_and_sigmoid(1, 1)
-        gate(0, 0)
-        sum_and_sigmoid(1, 0)
         gather_members(1, 2)
+        sum_on_tensor(0, 0, 4)
+        sum_on_tensor(0, 1, 5)
+        sum_on_tensor(0, 2, 6)
+        sum_on_vector(0, 3, ms_early[:])
+        sigmoid_and_back(0, 0, 0)
+        sum_on_tensor(1, 1, 4)
+        gather_members(1, 0)
+        sigmoid_and_back(0, 1, 1)
+        sigmoid_and_back(0, 2, 2)
+        sum_on_tensor(1, 2, 6)
+        sigmoid_in_place(0, 3, ms_early[:])
         gather_members(1, 3)
-        gate(0, 1)
-        gate(0, 2)
-        gate(0, 3)
-        w2_codes = reused.tile([P, N], U32, name="w2_codes", offset=0, align_bytes=64)
+        w2_grouped = keep.tile([P, N, PACK], BF16, name="w2_grouped", align_bytes=64)
+        nc.vector.tensor_copy(
+            w2_grouped[:].rearrange("p (c i) j -> p c j i", i=4), w2_raw[:].rearrange("p j (c i) -> p c j i", i=4)
+        )
+        gate(0, 0)
+        sum_on_vector(1, 0, ms_late[:, 0, :])
         nc.vector.quantize_mx(
             out=w2_codes[:].bitcast(FP8X4), scales=w2_plane[:], in_=w2_grouped[:].rearrange("p c j -> p (c j)")
         )
+        sigmoid_in_place(1, 0, ms_late[:, 0, :])
+        sigmoid_and_back(1, 1, 3)
+        sigmoid_and_back(1, 2, 7)
+        gate(0, 3)
+        sum_on_vector(1, 3, ms_late[:, 1, :])
+        sigmoid_in_place(1, 3, ms_late[:, 1, :])
+        gate(0, 1)
+        gate(0, 2)
+        gate(1, 0)
         interleave(0)
         gate(1, 1)
-        quantize_z(0)
-        second_product(0)
-        add_pairs(1, 2)
-        gate(1, 0)
-        sum_and_sigmoid(1, 2)
-        add_pairs(1, 3)
         gate(1, 2)
-        sum_and_sigmoid(1, 3)
         gate(1, 3)
+        quantize_z(0)
         interleave(1)
         quantize_z(1)
-        second_product(1)
-
-        bias = keep.tile([P, PACK], F32, name="bias")
-        nc.vector.scalar_tensor_tensor(bias[:], sl_t[:], -1.0, th_t[:], MULT, MULT)
-
-        old = reused.tile([P, PACK, S], F32, name="old", offset=4096, align_bytes=64)
+        for m in range(PACK):
+            rows = slice(m * P, (m + 1) * P)
+            h_banks[m] = psum.tile([P, S], F32, name="h_bank%d" % m, tag="bank%d" % (4 + m))
+            nc.tensor.matmul_mx(
+                out=h_banks[m][:],
+                lhsT=w2_codes[:, rows].bitcast(FP8X4),
+                lhsT_scale=w2_plane[:, rows],
+                rhs=z_codes[:].bitcast(FP8X4),
+                rhs_scale=z_plane[:],
+                start=True,
+                stop=True,
+            )
+        old = shared.tile([P, PACK, S], F32, name="old", offset=0, align_bytes=64)
         for m in range(PACK):
             nc.scalar.activation(old[:, m, :], page[m][:].indirect(n2_t[:]), COPY)
 
-        sg = [keep.tile([P, S], F32, name="sg%d" % m) for m in range(PACK)]
+        bias = keep.tile([P, PACK], F32, name="bias")
+        negated = keep.tile([P, PACK], F32, name="negated")
+        nc.gpsimd.tensor_scalar(negated[:], sl_t[:], -1.0, 0.0, MULT, ADD)
+        nc.gpsimd.tensor_tensor(bias[:], negated[:], th_t[:], MULT)
+
+        sg = {}
+        nw = {}
         change = [keep.tile([P, S], F32, name="change%d" % m) for m in range(PACK)]
-        gated = [keep.tile([P, S], F32, name="gated%d" % m) for m in range(PACK)]
-        nw = {m: keep.tile([P, S], F32, name="nw%d" % m) for m in (1, 2)}
-        for m in range(PACK):
-            if m == 1:
-                nc.vector.tensor_copy(h[m][:, :S], h_banks[m][:])
-            else:
-                nc.scalar.copy(h[m][:, :S], h_banks[m][:])
+        gated = {}
+
+        def gather_gate(m, tag):
+            sg[m] = reused.tile([P, S], F32, name="sg%d" % m, tag=tag)
             nc.scalar.activation(
                 sg[m][:], h[m][:].indirect(n3_t[:]), SIGMOID, bias=bias[:, m : m + 1], scale=sl_t[:, m : m + 1]
             )
@@ -257,9 +274,11 @@ def tile_picked_hashgsumgepg_none_p_kernel(
             nc.vector.tensor_tensor(change[m][:], h[m][:, :S], old[:, m, :], SUB)
 
         def apply_gate(m):
+            gated[m] = reused.tile([P, S], F32, name="gated%d" % m, tag="gated%d" % m)
             nc.vector.tensor_tensor(gated[m][:], sg[m][:], change[m][:], MULT)
 
         def add_old(m):
+            nw[m] = reused.tile([P, S], F32, name="nw%d" % m, tag="nw%d" % m)
             nc.vector.tensor_tensor(nw[m][:], gated[m][:], old[:, m, :], ADD)
 
         def scatter_and_store(m):
@@ -269,17 +288,21 @@ def tile_picked_hashgsumgepg_none_p_kernel(
                 nc.scalar.activation(page[m][:].indirect(n2_t[:]), nw[m][:], COPY)
             nc.sync.dma_start(out[m * P : (m + 1) * P, :], page[m][:])
 
-        subtract_old(0)
-        subtract_old(1)
+        nc.vector.tensor_copy(h[0][:, :S], h_banks[0][:])
+        nc.vector.tensor_copy(h[1][:, :S], h_banks[1][:])
+        nc.scalar.copy(h[2][:, :S], h_banks[2][:])
+        nc.scalar.copy(h[3][:, :S], h_banks[3][:])
+        for m in range(PACK):
+            gather_gate(m, "sg%d" % m)
+        for m in range(PACK):
+            subtract_old(m)
         apply_gate(0)
         apply_gate(1)
-        subtract_old(2)
-        add_old(1)
-        scatter_and_store(0)
-        scatter_and_store(1)
+        add_old(0)
         apply_gate(2)
-        subtract_old(3)
-        add_old(2)
+        add_old(1)
         apply_gate(3)
+        scatter_and_store(0)
         scatter_and_store(2)
+        scatter_and_store(1)
         scatter_and_store(3)

@@ -145,6 +145,15 @@ def tile_picked_hashgsumgepg_none_p_kernel(
             else:
                 nc.scalar.activation(members[half, t][:], looked_up, COPY)
 
+        def gather_last_members(part):
+            list_cols = HALF_ENTRIES // LIST_ROWS // 2
+            looked_up = y[PACK - 1][:].indirect(n1_t[:, (2 + part) * list_cols : (3 + part) * list_cols])
+            entries = slice(part * HALF_ENTRIES // 2, (part + 1) * HALF_ENTRIES // 2)
+            if part == 0:
+                nc.vector.tensor_copy(members[1, PACK - 1][:, entries], looked_up)
+            else:
+                nc.scalar.activation(members[1, PACK - 1][:, entries], looked_up, COPY)
+
         z_codes = keep.tile([P, S], U32, name="z_codes", align_bytes=64)
         z_plane = keep.tile([P, S], U8, name="z_plane", align_bytes=64)
         h_banks = {}
@@ -152,7 +161,7 @@ def tile_picked_hashgsumgepg_none_p_kernel(
         sig = {}
         sums = {}
         z_rows = [
-            shared.tile([P, PACK, HALF], BF16, name="z_rows%d" % half, offset=4096 + 1024 * half, align_bytes=64)
+            shared.tile([P, PACK - half, HALF], BF16, name="z_rows%d" % half, offset=4096 + 1024 * half, align_bytes=64)
             for half in range(2)
         ]
         z_grouped = [keep.tile([P, HALF, PACK], BF16, name="z_grouped%d" % half, align_bytes=64) for half in range(2)]
@@ -180,12 +189,14 @@ def tile_picked_hashgsumgepg_none_p_kernel(
 
         def gate(half, t):
             cols = slice(half * HALF, (half + 1) * HALF)
-            nc.vector.scalar_tensor_tensor(
-                z_rows[half][:, t, :], y[t][:, cols], gn_t[:, t : t + 1], sig[half, t][:], MULT, MULT
-            )
+            z = z_grouped[half][:, :, t] if (half, t) == (1, PACK - 1) else z_rows[half][:, t, :]
+            nc.vector.scalar_tensor_tensor(z, y[t][:, cols], gn_t[:, t : t + 1], sig[half, t][:], MULT, MULT)
 
         def interleave(half):
-            nc.vector.tensor_copy(z_grouped[half][:], z_rows[half][:].rearrange("p t j -> p j t"))
+            if half == 0:
+                nc.scalar.copy(z_grouped[0][:], z_rows[0][:].rearrange("p t j -> p j t"))
+            else:
+                nc.vector.tensor_copy(z_grouped[1][:, :, : PACK - 1], z_rows[1][:].rearrange("p t j -> p j t"))
 
         def quantize_z(half):
             cols = slice(half * HALF, (half + 1) * HALF)
@@ -201,6 +212,8 @@ def tile_picked_hashgsumgepg_none_p_kernel(
             gather_members(0, t)
         gather_members(1, 1)
         gather_members(1, 2)
+        members[1, PACK - 1] = keep.tile([P, HALF_ENTRIES], F32, name="members_last")
+        gather_last_members(0)
         sum_on_tensor(0, 0, 4)
         sum_on_tensor(0, 1, 5)
         sum_on_tensor(0, 2, 6)
@@ -212,11 +225,9 @@ def tile_picked_hashgsumgepg_none_p_kernel(
         sigmoid_and_back(0, 2, 2)
         sum_on_tensor(1, 2, 6)
         sigmoid_in_place(0, 3, ms_early[:])
-        gather_members(1, 3)
+        gather_last_members(1)
         w2_grouped = keep.tile([P, N, PACK], BF16, name="w2_grouped", align_bytes=64)
-        nc.vector.tensor_copy(
-            w2_grouped[:].rearrange("p (c i) j -> p c j i", i=4), w2_raw[:].rearrange("p j (c i) -> p c j i", i=4)
-        )
+        nc.gpsimd.tensor_scalar(w2_grouped[:], w2_raw[:].rearrange("p j c -> p c j"), 1.0, 0.0, MULT, ADD)
         gate(0, 0)
         sum_on_vector(1, 0, ms_late[:, 0, :])
         nc.vector.quantize_mx(
@@ -226,17 +237,17 @@ def tile_picked_hashgsumgepg_none_p_kernel(
         sigmoid_and_back(1, 1, 3)
         sigmoid_and_back(1, 2, 7)
         gate(0, 3)
-        sum_on_vector(1, 3, ms_late[:, 1, :])
-        sigmoid_in_place(1, 3, ms_late[:, 1, :])
         gate(0, 1)
         gate(0, 2)
-        gate(1, 0)
         interleave(0)
+        sum_on_vector(1, 3, ms_late[:, 1, :])
+        sigmoid_in_place(1, 3, ms_late[:, 1, :])
+        gate(1, 0)
         gate(1, 1)
         gate(1, 2)
+        interleave(1)
         gate(1, 3)
         quantize_z(0)
-        interleave(1)
         quantize_z(1)
         for m in range(PACK):
             rows = slice(m * P, (m + 1) * P)

from contextlib import ExitStack

import concourse.mybir as mybir
from concourse.masks import make_identity

K, T, S, N, H, W, U = 512, 2048, 256, 512, 512, 1024, 1024
FLOPS = 2 * K * H * S + 2 * H * N * S

F32 = mybir.dt.float32
BF16 = mybir.dt.bfloat16
I32 = mybir.dt.int32
U32 = mybir.dt.uint32
U16 = mybir.dt.uint16
U8 = mybir.dt.uint8
FP8X4 = mybir.dt.float8_e4m3fn_x4
ADD = mybir.AluOpType.add
SUB = mybir.AluOpType.subtract
MULT = mybir.AluOpType.mult
AXIS_X = mybir.AxisListType.X
COPY = mybir.ActivationFunctionType.Copy
SIGMOID = mybir.ActivationFunctionType.Sigmoid

P = 128
PACK = 4
MEMBERS = 4
HALF = S // 2
HALF_ENTRIES = HALF * MEMBERS
LIST_ROWS = 16
Y_WINDOW = HALF_ENTRIES + LIST_ROWS
H_WINDOW = 2 * S
VECTOR_GATHERS = ((0, 1), (1, 1), (1, 2))
W1_VECTOR_SHARE = 88
X_CODES_AT = 16384 + 64 + 4096 + 4096 - 256
VECTOR_SCATTER_TILES = (2, 3)


def tile_picked_hashgsumgepg_none_p_kernel(
    tc, x_words, x_scales, w1, gn, w2, mem, sl, th, offs, n1, n2, n3, out
):
    nc = tc.nc
    with ExitStack() as ctx:
        keep = ctx.enter_context(tc.tile_pool(name="keep", bufs=1))
        shared = ctx.enter_context(tc.tile_pool(name="shared", bufs=1))
        reused = ctx.enter_context(tc.tile_pool(name="reused", bufs=1))
        psum = ctx.enter_context(tc.psum_pool(name="psum", bufs=1))

        offs_t = keep.tile([P, S // LIST_ROWS], U16, name="offs_t")
        n1_t = keep.tile([P, W // LIST_ROWS], U16, name="n1_t")
        n2_t = keep.tile([P, S // LIST_ROWS], U16, name="n2_t")
        n3_t = keep.tile([P, S // LIST_ROWS], U16, name="n3_t")

        w1_raw = shared.tile([P, PACK, H], F32, name="w1_raw", offset=0, align_bytes=64)
        x_window = shared.tile([P, T], U32, name="x_window", offset=8192, align_bytes=64)
        scale_window = keep.tile([P, T], U8, name="scale_window", align_bytes=64)
        picked_scales = shared.tile([P, S], U8, name="picked_scales", offset=16384, align_bytes=64)

        warm_in = keep.tile([P, 1], F32, name="warm_in")
        warm_out = keep.tile([P, 1], F32, name="warm_out")
        nc.gpsimd.memset(warm_in[:], 0.0)
        nc.scalar.activation(warm_out[:], warm_in[:], SIGMOID)

        nc.sync.dma_start(offs_t[:], offs)
        nc.sync.dma_start(
            scale_window[:].bitcast(I32), x_scales[0].bitcast(I32).unsqueeze(1).to_broadcast([16, 8, T // 4])
        )
        nc.sync.dma_start(w1_raw[:], w1.rearrange("(p j) c -> p j c", j=PACK))
        nc.sync.dma_start(x_window[:].bitcast(I32), x_words[0].rearrange("p n t -> p (n t)").bitcast(I32))
        nc.sync.dma_start(n1_t[:], n1)
        nc.sync.dma_start(n2_t[:], n2)
        nc.sync.dma_start(n3_t[:], n3)

        identity = keep.tile([P, P], F32, name="identity")
        make_identity(nc, identity[:])

        y = [keep.tile([P, Y_WINDOW], F32, name="y%d" % t) for t in range(PACK)]
        h = [keep.tile([P, H_WINDOW], F32, name="h%d" % m) for m in range(PACK)]

        for t in range(PACK):
            nc.vector.memset(y[t][:, S:], 0.0)
        for m in range(PACK):
            nc.vector.memset(h[m][:, S:], 0.0)

        nc.vector.tensor_copy(picked_scales[:], scale_window[:].indirect(offs_t[:]))
        x_plane = keep.tile([P, S], U8, name="x_plane", align_bytes=64)
        nc.vector.tensor_copy(x_plane[:].bitcast(I32), picked_scales[:].bitcast(I32))
        for c in range(1, 4):
            nc.scalar.dma_start(x_plane[c:P:32, :].bitcast(I32), picked_scales[8 * c : P : 32, :].bitcast(I32))

        w1_grouped = keep.tile([P, PACK * H], BF16, name="w1_grouped", align_bytes=64)
        dealt = w1_grouped[:].rearrange("p (t m j) -> p m t j", t=PACK, j=PACK)
        source = w1_raw[:].rearrange("p j (m t) -> p m t j", t=PACK)
        nc.vector.tensor_copy(dealt[:, :W1_VECTOR_SHARE], source[:, :W1_VECTOR_SHARE])
        nc.scalar.copy(dealt[:, W1_VECTOR_SHARE:], source[:, W1_VECTOR_SHARE:])
        w1_codes = keep.tile([P, H], U32, name="w1_codes", align_bytes=64)
        w1_plane = keep.tile([P, H], U8, name="w1_plane", align_bytes=64)
        nc.vector.quantize_mx(out=w1_codes[:].bitcast(FP8X4), scales=w1_plane[:], in_=w1_grouped[:])

        x_codes = shared.tile([P, S], U32, name="x_codes", offset=X_CODES_AT, align_bytes=64)
        nc.vector.tensor_copy(x_codes[:], x_window[:].indirect(offs_t[:]))

        gn_t = shared.tile([P, PACK], F32, name="gn_t", offset=16384, align_bytes=64)
        sl_t = shared.tile([P, PACK], F32, name="sl_t", offset=X_CODES_AT + 256, align_bytes=64)
        th_t = shared.tile([P, PACK], F32, name="th_t", offset=X_CODES_AT + 320, align_bytes=64)
        w2_raw = shared.tile([P, PACK, N], F32, name="w2_raw", offset=0, align_bytes=64)
        page_offsets = (16384 + 64, 8192, 12288, X_CODES_AT + 256 - 4096)
        page = [
            shared.tile([P, U], F32, name="page%d" % m, offset=page_offsets[m], align_bytes=64) for m in range(PACK)
        ]
        nc.sync.dma_start(w2_raw[:], w2.rearrange("(p j) c -> p j c", j=PACK))
        nc.sync.dma_start(gn_t[:], gn.rearrange("(p t) o -> p (t o)", t=PACK))
        for m in range(PACK):
            nc.sync.dma_start(page[m][:], mem[m * P : (m + 1) * P, :])
        with nc.allow_non_contiguous_dma(reason="one value a row of h"):
            nc.sync.dma_start(sl_t[:], sl.rearrange("(m p) o -> p (m o)", p=P))
            nc.sync.dma_start(th_t[:], th.rearrange("(m p) o -> p (m o)", p=P))

        for t in range(PACK):
            cols = slice(t * P, (t + 1) * P)
            y_bank = psum.tile([P, S], F32, name="y_bank%d" % t, tag="bank%d" % t)
            nc.tensor.matmul_mx(
                out=y_bank[:],
                lhsT=w1_codes[:, cols].bitcast(FP8X4),
                lhsT_scale=w1_plane[:, cols],
                rhs=x_codes[:].bitcast(FP8X4),
                rhs_scale=x_plane[:],
                start=True,
                stop=True,
            )
            if t % 2 == 0:
                nc.scalar.copy(y[t][:, :S], y_bank[:])
            else:
                nc.vector.tensor_copy(y[t][:, :S], y_bank[:])

        w2_codes = keep.tile([P, N], U32, name="w2_codes", align_bytes=64)
        w2_plane = keep.tile([P, N], U8, name="w2_plane", align_bytes=64)

        members = {}

        def gather_members(half, t):
            list_cols = HALF_ENTRIES // LIST_ROWS
            members[half, t] = keep.tile([P, HALF_ENTRIES], F32, name="members%d_%d" % (half, t))
            looked_up = y[t][:].indirect(n1_t[:, half * list_cols : (half + 1) * list_cols])
            if (half, t) in VECTOR_GATHERS:
                nc.vector.tensor_copy(members[half, t][:], looked_up)
            else:
                nc.scalar.activation(members[half, t][:], looked_up, COPY)

        def gather_last_members(part):
            list_cols = HALF_ENTRIES // LIST_ROWS // 2
            looked_up = y[PACK - 1][:].indirect(n1_t[:, (2 + part) * list_cols : (3 + part) * list_cols])
            entries = slice(part * HALF_ENTRIES // 2, (part + 1) * HALF_ENTRIES // 2)
            if part == 0:
                nc.vector.tensor_copy(members[1, PACK - 1][:, entries], looked_up)
            else:
                nc.scalar.activation(members[1, PACK - 1][:, entries], looked_up, COPY)

        z_codes = keep.tile([P, S], U32, name="z_codes", align_bytes=64)
        z_plane = keep.tile([P, S], U8, name="z_plane", align_bytes=64)
        h_banks = {}

        sig = {}
        sums = {}
        z_rows = [
            shared.tile([P, PACK - half, HALF], BF16, name="z_rows%d" % half, offset=4096 + 1024 * half, align_bytes=64)
            for half in range(2)
        ]
        z_grouped = [keep.tile([P, HALF, PACK], BF16, name="z_grouped%d" % half, align_bytes=64) for half in range(2)]

        def sum_on_vector(half, t, ms):
            nc.vector.tensor_reduce(ms, members[half, t][:].rearrange("p (j a) -> p j a", a=MEMBERS), AXIS_X, ADD)

        def sigmoid_in_place(half, t, ms):
            sig[half, t] = keep.tile([P, HALF], F32, name="sig%d_%d" % (half, t))
            nc.scalar.activation(sig[half, t][:], ms, SIGMOID)

        def sum_on_tensor(half, t, bank):
            sums[half, t] = psum.tile([P, P], F32, name="sum%d_%d" % (half, t), tag="bank%d" % bank)
            by_member = members[half, t][:].rearrange("p (j a) -> p a j", a=MEMBERS)
            for a in range(MEMBERS):
                nc.tensor.matmul(
                    sums[half, t][:], by_member[:, a, :], identity[:], start=a == 0, stop=a == MEMBERS - 1, is_transpose=True
                )

        def sigmoid_and_back(half, t, bank):
            turned = keep.tile([P, P], F32, name="turned%d_%d" % (half, t))
            nc.scalar.activation(turned[:], sums[half, t][:], SIGMOID)
            sig[half, t] = psum.tile([P, HALF], F32, name="sig%d_%d" % (half, t), tag="bank%d" % bank)
            nc.tensor.transpose(sig[half, t][:], turned[:], identity[:])

        def gate(half, t):
            cols = slice(half * HALF, (half + 1) * HALF)
            z = z_grouped[half][:, :, t] if (half, t) == (1, PACK - 1) else z_rows[half][:, t, :]
            nc.vector.scalar_tensor_tensor(z, y[t][:, cols], gn_t[:, t : t + 1], sig[half, t][:], MULT, MULT)

        def interleave(half):
            if half == 0:
                nc.scalar.copy(z_grouped[0][:], z_rows[0][:].rearrange("p t j -> p j t"))
            else:
                nc.vector.tensor_copy(z_grouped[1][:, :, : PACK - 1], z_rows[1][:].rearrange("p t j -> p j t"))

        def quantize_z(half):
            cols = slice(half * HALF, (half + 1) * HALF)
            nc.vector.quantize_mx(
                out=z_codes[:, cols].bitcast(FP8X4),
                scales=z_plane[:, cols],
                in_=z_grouped[half][:].rearrange("p j t -> p (j t)"),
            )

        ms_early = keep.tile([P, HALF], F32, name="ms_early")
        ms_late = shared.tile([P, 2, HALF], F32, name="ms_late", offset=0, align_bytes=64)
        for t in range(PACK):
            gather_members(0, t)
        gather_members(1, 1)
        gather_members(1, 2)
        members[1, PACK - 1] = keep.tile([P, HALF_ENTRIES], F32, name="members_last")
        gather_last_members(0)
        sum_on_tensor(0, 0, 4)
        sum_on_tensor(0, 1, 5)
        sum_on_tensor(0, 2, 6)
        sum_on_vector(0, 3, ms_early[:])
        sigmoid_and_back(0, 0, 0)
        sum_on_tensor(1, 1, 4)
        gather_members(1, 0)
        sigmoid_and_back(0, 1, 1)
        sigmoid_and_back(0, 2, 2)
        sum_on_tensor(1, 2, 6)
        sigmoid_in_place(0, 3, ms_early[:])
        gather_last_members(1)
        w2_grouped = keep.tile([P, N, PACK], BF16, name="w2_grouped", align_bytes=64)
        nc.gpsimd.tensor_scalar(w2_grouped[:], w2_raw[:].rearrange("p j c -> p c j"), 1.0, 0.0, MULT, ADD)
        gate(0, 0)
        sum_on_vector(1, 0, ms_late[:, 0, :])
        nc.vector.quantize_mx(
            out=w2_codes[:].bitcast(FP8X4), scales=w2_plane[:], in_=w2_grouped[:].rearrange("p c j -> p (c j)")
        )
        sigmoid_in_place(1, 0, ms_late[:, 0, :])
        sigmoid_and_back(1, 1, 3)
        sigmoid_and_back(1, 2, 7)
        gate(0, 3)
        gate(0, 1)
        gate(0, 2)
        interleave(0)
        sum_on_vector(1, 3, ms_late[:, 1, :])
        sigmoid_in_place(1, 3, ms_late[:, 1, :])
        gate(1, 0)
        gate(1, 1)
        gate(1, 2)
        interleave(1)
        gate(1, 3)
        quantize_z(0)
        quantize_z(1)
        for m in range(PACK):
            rows = slice(m * P, (m + 1) * P)
            h_banks[m] = psum.tile([P, S], F32, name="h_bank%d" % m, tag="bank%d" % (4 + m))
            nc.tensor.matmul_mx(
                out=h_banks[m][:],
                lhsT=w2_codes[:, rows].bitcast(FP8X4),
                lhsT_scale=w2_plane[:, rows],
                rhs=z_codes[:].bitcast(FP8X4),
                rhs_scale=z_plane[:],
                start=True,
                stop=True,
            )
        old = shared.tile([P, PACK, S], F32, name="old", offset=0, align_bytes=64)
        for m in range(PACK):
            nc.scalar.activation(old[:, m, :], page[m][:].indirect(n2_t[:]), COPY)

        bias = keep.tile([P, PACK], F32, name="bias")
        negated = keep.tile([P, PACK], F32, name="negated")
        nc.gpsimd.tensor_scalar(negated[:], sl_t[:], -1.0, 0.0, MULT, ADD)
        nc.gpsimd.tensor_tensor(bias[:], negated[:], th_t[:], MULT)

        sg = {}
        nw = {}
        change = [keep.tile([P, S], F32, name="change%d" % m) for m in range(PACK)]
        gated = {}

        def gather_gate(m, tag):
            sg[m] = reused.tile([P, S], F32, name="sg%d" % m, tag=tag)
            nc.scalar.activation(
                sg[m][:], h[m][:].indirect(n3_t[:]), SIGMOID, bias=bias[:, m : m + 1], scale=sl_t[:, m : m + 1]
            )

        def subtract_old(m):
            nc.vector.tensor_tensor(change[m][:], h[m][:, :S], old[:, m, :], SUB)

        def apply_gate(m):
            gated[m] = reused.tile([P, S], F32, name="gated%d" % m, tag="gated%d" % m)
            nc.vector.tensor_tensor(gated[m][:], sg[m][:], change[m][:], MULT)

        def add_old(m):
            nw[m] = reused.tile([P, S], F32, name="nw%d" % m, tag="nw%d" % m)
            nc.vector.tensor_tensor(nw[m][:], gated[m][:], old[:, m, :], ADD)

        def scatter_and_store(m):
            if m in VECTOR_SCATTER_TILES:
                nc.vector.tensor_tensor(page[m][:].indirect(n2_t[:]), gated[m][:], old[:, m, :], ADD)
            else:
                nc.scalar.activation(page[m][:].indirect(n2_t[:]), nw[m][:], COPY)
            nc.sync.dma_start(out[m * P : (m + 1) * P, :], page[m][:])

        nc.vector.tensor_copy(h[0][:, :S], h_banks[0][:])
        nc.vector.tensor_copy(h[1][:, :S], h_banks[1][:])
        nc.scalar.copy(h[2][:, :S], h_banks[2][:])
        nc.scalar.copy(h[3][:, :S], h_banks[3][:])
        for m in range(PACK):
            gather_gate(m, "sg%d" % m)
        for m in range(PACK):
            subtract_old(m)
        apply_gate(0)
        apply_gate(1)
        add_old(0)
        apply_gate(2)
        add_old(1)
        apply_gate(3)
        scatter_and_store(0)
        scatter_and_store(2)
        scatter_and_store(1)
        scatter_and_store(3)
